import numpy as np
import ml_dtypes

BF16 = ml_dtypes.bfloat16


def bf(x):
    return np.asarray(x, np.float32).astype(BF16)


def f32(x):
    return np.asarray(x, np.float32)


def f64(x):
    return np.asarray(x).astype(np.float64)


def striped(idx):
    return np.tile(idx.reshape(-1, 16).T, (8, 1))


S, K, H, M, N, D, V = 2048, 128, 128, 128, 512, 8, 64


def gelu_tanh(v):
    return 0.5 * v * (1.0 + np.tanh(np.sqrt(2.0 / np.pi) * (v + 0.044715 * v**3)))


def setup_inputs():
    return {"x": bf(np.random.standard_normal((K, S))), "w": bf(np.random.standard_normal((K, H)) / np.sqrt(K)), "b": f32(0.5 * np.random.standard_normal((H, 1))), "w2": bf(np.random.standard_normal((H, M)) / np.sqrt(H)), "offs": striped(np.random.permutation(S)[:N])}


def reference(x, w, b, w2, offs):
    idx = offs[:16].T.reshape(-1)
    t = gelu_tanh(f64(w).T @ f64(x) + f64(b))
    return (f64(w2).T @ t[:, idx]).reshape(M, V, D).max(axis=2)

@@ -1,0 +1,51 @@
+import concourse.mybir as mybir
+
+P = 128
+S = 2048
+N = 512
+D = 8
+BANK = 512
+
+FLOPS = 2 * P * P * S + 2 * P * P * N
+
+BF16, F32, U16 = mybir.dt.bfloat16, mybir.dt.float32, mybir.dt.uint16
+GELU = mybir.ActivationFunctionType.Gelu_apprx_tanh
+
+
+def tile_rows_gcn2_gelu_max_kernel(tc, x, w, b, w2, offs, out):
+    nc = tc.nc
+    with (
+        tc.tile_pool(name="held", bufs=1) as held,
+        tc.psum_pool(name="psum", bufs=1) as psum,
+    ):
+        w_sb = held.tile([P, P], BF16, name="w_sb")
+        b_sb = held.tile([P, 1], F32, name="b_sb")
+        w2_sb = held.tile([P, P], BF16, name="w2_sb")
+        offsets = held.tile([P, N // 16], U16, name="offsets")
+        x_sb = held.tile([P, S], BF16, name="x_sb")
+        h = held.tile([P, S], BF16, name="h")
+        pooled = held.tile([P, N // D], F32, name="pooled")
+
+        nc.scalar.dma_start(b_sb[:], b)
+        nc.sync.dma_start(w_sb[:], w)
+        for c in range(S // BANK):
+            cols = slice(c * BANK, (c + 1) * BANK)
+            nc.sync.dma_start(x_sb[:, cols], x[:, cols])
+        nc.sync.dma_start(w2_sb[:], w2)
+        nc.sync.dma_start(offsets[:], offs)
+
+        for c in range(S // BANK):
+            cols = slice(c * BANK, (c + 1) * BANK)
+            pre = psum.tile([P, BANK], F32, name=f"pre{c}")
+            nc.tensor.matmul(pre[:], w_sb[:], x_sb[:, cols], start=True, stop=True)
+            nc.scalar.activation(h[:, cols], pre[:], GELU, bias=b_sb[:])
+
+        picked = psum.tile([P, N], F32, name="picked")
+        nc.tensor.matmul(picked[:], w2_sb[:], h[:].indirect(offsets[:]), start=True, stop=True)
+        nc.vector.tensor_reduce(
+            pooled[:],
+            picked[:].rearrange("p (v t) -> p v t", t=D),
+            mybir.AxisListType.X,
+            mybir.AluOpType.max,
+        )
+        nc.sync.dma_start(out, pooled[:])

@@ -26,7 +26,12 @@ def tile_rows_gcn2_gelu_max_kernel(tc, x, w, b, w2, offs, out):
         h = held.tile([P, S], BF16, name="h")
         pooled = held.tile([P, N // D], F32, name="pooled")
 
+        warm = held.tile([P, 1], F32, name="warm")
+
         nc.scalar.dma_start(b_sb[:], b)
+        nc.vector.memset(warm[:], 0.0)
+        nc.scalar.activation(warm[:], warm[:], GELU)
+
         nc.sync.dma_start(w_sb[:], w)
         for c in range(S // BANK):
             cols = slice(c * BANK, (c + 1) * BANK)

@@ -4,7 +4,10 @@ P = 128
 S = 2048
 N = 512
 D = 8
-BANK = 512
+STEP = 256
+LOADS = (256, 256, 512, 1024)
+PARTS = 4
+PART = N // PARTS
 
 FLOPS = 2 * P * P * S + 2 * P * P * N
 
@@ -16,7 +19,8 @@ def tile_rows_gcn2_gelu_max_kernel(tc, x, w, b, w2, offs, out):
     nc = tc.nc
     with (
         tc.tile_pool(name="held", bufs=1) as held,
-        tc.psum_pool(name="psum", bufs=1) as psum,
+        tc.psum_pool(name="layer1", bufs=4) as layer1,
+        tc.psum_pool(name="layer2", bufs=PARTS) as layer2,
     ):
         w_sb = held.tile([P, P], BF16, name="w_sb")
         b_sb = held.tile([P, 1], F32, name="b_sb")
@@ -25,32 +29,34 @@ def tile_rows_gcn2_gelu_max_kernel(tc, x, w, b, w2, offs, out):
         x_sb = held.tile([P, S], BF16, name="x_sb")
         h = held.tile([P, S], BF16, name="h")
         pooled = held.tile([P, N // D], F32, name="pooled")
-
         warm = held.tile([P, 1], F32, name="warm")
 
+        nc.scalar.dma_start(w_sb[:], w)
         nc.scalar.dma_start(b_sb[:], b)
         nc.vector.memset(warm[:], 0.0)
         nc.scalar.activation(warm[:], warm[:], GELU)
 
-        nc.sync.dma_start(w_sb[:], w)
-        for c in range(S // BANK):
-            cols = slice(c * BANK, (c + 1) * BANK)
-            nc.sync.dma_start(x_sb[:, cols], x[:, cols])
+        first = 0
+        for width in LOADS:
+            nc.sync.dma_start(x_sb[:, first : first + width], x[:, first : first + width])
+            first += width
         nc.sync.dma_start(w2_sb[:], w2)
         nc.sync.dma_start(offsets[:], offs)
 
-        for c in range(S // BANK):
-            cols = slice(c * BANK, (c + 1) * BANK)
-            pre = psum.tile([P, BANK], F32, name=f"pre{c}")
+        for c in range(S // STEP):
+            cols = slice(c * STEP, (c + 1) * STEP)
+            pre = layer1.tile([P, STEP], F32, name="pre")
             nc.tensor.matmul(pre[:], w_sb[:], x_sb[:, cols], start=True, stop=True)
             nc.scalar.activation(h[:, cols], pre[:], GELU, bias=b_sb[:])
 
-        picked = psum.tile([P, N], F32, name="picked")
-        nc.tensor.matmul(picked[:], w2_sb[:], h[:].indirect(offsets[:]), start=True, stop=True)
-        nc.vector.tensor_reduce(
-            pooled[:],
-            picked[:].rearrange("p (v t) -> p v t", t=D),
-            mybir.AxisListType.X,
-            mybir.AluOpType.max,
-        )
+        for q in range(PARTS):
+            picked = layer2.tile([P, PART], F32, name="picked")
+            entries = offsets[:, q * PART // 16 : (q + 1) * PART // 16]
+            nc.tensor.matmul(picked[:], w2_sb[:], h[:].indirect(entries), start=True, stop=True)
+            nc.vector.tensor_reduce(
+                pooled[:, q * PART // D : (q + 1) * PART // D],
+                picked[:].rearrange("p (v t) -> p v t", t=D),
+                mybir.AxisListType.X,
+                mybir.AluOpType.max,
+            )
         nc.sync.dma_start(out, pooled[:])

@@ -5,7 +5,8 @@ S = 2048
 N = 512
 D = 8
 STEP = 256
-LOADS = (256, 256, 512, 1024)
+STEPS = (STEP // 2, STEP // 2) + (STEP,) * (S // STEP - 1)
+LOADS = (256, 256, 512, 512, 512)
 PARTS = 4
 PART = N // PARTS
 
@@ -43,9 +44,11 @@ def tile_rows_gcn2_gelu_max_kernel(tc, x, w, b, w2, offs, out):
         nc.sync.dma_start(w2_sb[:], w2)
         nc.sync.dma_start(offsets[:], offs)
 
-        for c in range(S // STEP):
-            cols = slice(c * STEP, (c + 1) * STEP)
-            pre = layer1.tile([P, STEP], F32, name="pre")
+        first = 0
+        for width in STEPS:
+            cols = slice(first, first + width)
+            first += width
+            pre = layer1.tile([P, width], F32, name="pre")
             nc.tensor.matmul(pre[:], w_sb[:], x_sb[:, cols], start=True, stop=True)
             nc.scalar.activation(h[:, cols], pre[:], GELU, bias=b_sb[:])
 

import concourse.mybir as mybir

P = 128
S = 2048
N = 512
D = 8
STEP = 256
STEPS = (STEP // 2, STEP // 2) + (STEP,) * (S // STEP - 1)
LOADS = (256, 256, 512, 512, 512)
PARTS = 4
PART = N // PARTS

FLOPS = 2 * P * P * S + 2 * P * P * N

BF16, F32, U16 = mybir.dt.bfloat16, mybir.dt.float32, mybir.dt.uint16
GELU = mybir.ActivationFunctionType.Gelu_apprx_tanh


def tile_rows_gcn2_gelu_max_kernel(tc, x, w, b, w2, offs, out):
    nc = tc.nc
    with (
        tc.tile_pool(name="held", bufs=1) as held,
        tc.psum_pool(name="layer1", bufs=4) as layer1,
        tc.psum_pool(name="layer2", bufs=PARTS) as layer2,
    ):
        w_sb = held.tile([P, P], BF16, name="w_sb")
        b_sb = held.tile([P, 1], F32, name="b_sb")
        w2_sb = held.tile([P, P], BF16, name="w2_sb")
        offsets = held.tile([P, N // 16], U16, name="offsets")
        x_sb = held.tile([P, S], BF16, name="x_sb")
        h = held.tile([P, S], BF16, name="h")
        pooled = held.tile([P, N // D], F32, name="pooled")
        warm = held.tile([P, 1], F32, name="warm")

        nc.scalar.dma_start(w_sb[:], w)
        nc.scalar.dma_start(b_sb[:], b)
        nc.vector.memset(warm[:], 0.0)
        nc.scalar.activation(warm[:], warm[:], GELU)

        first = 0
        for width in LOADS:
            nc.sync.dma_start(x_sb[:, first : first + width], x[:, first : first + width])
            first += width
        nc.sync.dma_start(w2_sb[:], w2)
        nc.sync.dma_start(offsets[:], offs)

        first = 0
        for width in STEPS:
            cols = slice(first, first + width)
            first += width
            pre = layer1.tile([P, width], F32, name="pre")
            nc.tensor.matmul(pre[:], w_sb[:], x_sb[:, cols], start=True, stop=True)
            nc.scalar.activation(h[:, cols], pre[:], GELU, bias=b_sb[:])

        for q in range(PARTS):
            picked = layer2.tile([P, PART], F32, name="picked")
            entries = offsets[:, q * PART // 16 : (q + 1) * PART // 16]
            nc.tensor.matmul(picked[:], w2_sb[:], h[:].indirect(entries), start=True, stop=True)
            nc.vector.tensor_reduce(
                pooled[:, q * PART // D : (q + 1) * PART // D],
                picked[:].rearrange("p (v t) -> p v t", t=D),
                mybir.AxisListType.X,
                mybir.AluOpType.max,
            )
        nc.sync.dma_start(out, pooled[:])
